import numpy as np, ml_dtypes
CORES = [78,86,94,102,110,118]
N = 6
import mx_ref
NC = 128
BF = ml_dtypes.bfloat16
def cut(t, i, w=512):
    return t[:, w * i:w * i + w]
def term(a, B):
    return np.stack([mx_ref.matmul(mx_ref.quantize(cut(a, i)), B) for i in range(4)], axis=2).reshape(128, -1)
def setup_inputs(rng):
    def f(*shape):
        return mx_ref.flush((rng.standard_normal(shape, dtype=np.float32) * np.exp2(rng.integers(-2, 3, shape[:-1] + (1,)))).astype(BF))
    return {"a": f(N, 128, 4 * 512), "b": f(N, 128, 2 * 4 * NC)}
def setup_inputs_blocks(rng):
    d = setup_inputs(rng)
    for k in ("a", "b"): d[k] = mx_ref.spread(d[k], rng, 2)
    return d
def setup_inputs_wide(rng):
    d = setup_inputs(rng)
    for k in ("a", "b"): d[k] = mx_ref.flush((d[k].astype(np.float32) * np.exp2(rng.integers(-4, 5, (N, 1, 1))).astype(np.float32)).astype(BF))
    return d
def setup_inputs_lossless(rng):
    a = np.zeros((N, 128, 4 * 128, 4), np.float32)
    for r in range(N):
        k = rng.integers(0, 512, size=4 * 128)
        a[r, k // 4, np.arange(4 * 128), k % 4] = 1.0
    size = np.tile(np.repeat(2.0 ** rng.integers(-4, 5, size=(1, 1, NC)), 4, axis=2), (1, 1, 2))
    b = rng.integers(-1, 2, size=(N, 128, 2 * 4 * NC)) * size
    return {"a": a.reshape(N, 128, 4 * 512).astype(BF), "b": b.astype(np.float32).astype(BF)}
def reference(a, b):
    T = [term(a[r], mx_ref.quantize(cut(b[r], k, 4 * NC))) for r in range(N) for k in range(2)]
    y = np.zeros((N, 128, 4 * NC), np.float32)
    for c in range(N):
        y[c] = mx_ref.total(T[:2 * c + 2])
    return {"y": y}

from concourse.bass import DstId, RemoteDMATransfer
from concourse.mybir import dt, AluOpType, ActivationFunctionType

N_TILES = 4
W = 128
E = N_TILES * W
ZW = E + 4
BANK = 512

SEND_R = {0: [[2], [1, 3, 4]], 1: [[2], [3, 4]], 2: [[3]], 3: [[5]], 4: [[5]]}
HUB = {2: ([1, 0], 5), 3: ([2], 4)}
LAST = {0: [], 1: [0], 2: [1, 0], 3: [2, 1, 0], 4: [1, 0, "s"], 5: [3, 4, "s"]}

SCRATCH = {
    "at": ("sbuf", [128, 4 * E], "bfloat16"),
    "bt": ("sbuf", [128, 2 * E], "bfloat16"),
    "z": ("sbuf", [128, ZW], "bfloat16"),
    "aq": ("sbuf", [128, 4 * W], "float8_e4m3fn_x4"),
    "asc": ("sbuf", [128, 4 * W], "uint8"),
    "bq": ("sbuf", [128, 2 * W], "float8_e4m3fn_x4"),
    "bsc": ("sbuf", [128, 2 * W], "uint8"),
    "wq": ("sbuf", [128, 4 * W], "float8_e4m3fn_x4"),
    "wsc": ("sbuf", [128, 4 * W], "uint8"),
    "h": ("sbuf", [128, E], "bfloat16"),
    "hq": ("sbuf", [128, W], "float8_e4m3fn_x4"),
    "hsc": ("sbuf", [128, W], "uint8"),
    "h2": ("sbuf", [128, E], "bfloat16"),
    "h2q": ("sbuf", [128, W], "float8_e4m3fn_x4"),
    "h2sc": ("sbuf", [128, W], "uint8"),
    "ysb": ("sbuf", [128, E], "float32"),
    "ps0": ("psum", [128, 4 * BANK], "float32"),
    "ps1": ("psum", [128, 4 * BANK], "float32"),
}
for _k in (0, 1, 2, 3, 4, "s"):
    SCRATCH["rq%s" % _k] = ("sbuf", [128, W], "float8_e4m3fn_x4")
    SCRATCH["rsc%s" % _k] = ("sbuf", [128, W], "uint8")
SEMAPHORES = ["sent", "ldb", "lda0", "lda1", "stored"] + ["arr%s" % k for k in (0, 1, 2, 3, 4, "s")] \
    + ["e%d" % k for k in range(60)]


def rank_program(g, core, T, topo):
    rank = T.rank_of(core)
    if rank is None:
        return
    vec, ten, sca, syn = g.vector, g.tensor, g.scalar, g.sync
    used = [0]
    sent = [0]

    def event():
        used[0] += 1
        return T.sem["e%d" % (used[0] - 1)]

    def cols(i):
        return slice(W * i, W * i + W)

    def bank(ps, t):
        return ps[:, BANK * t:BANK * t + W]

    syn.dma_start(T.bt[:], T.b[:]).then_inc(T.sem.ldb, 16)
    sca.dma_start(T.at[:, 0:3 * E], T.a[:, 0:3 * E]).then_inc(T.sem.lda0, 16)
    syn.dma_start(T.at[:, 3 * E:4 * E], T.a[:, 3 * E:4 * E]).then_inc(T.sem.lda1, 16)

    tiles_in = LAST[rank]
    w_ready = []
    if tiles_in:
        e_one, e_diag = event(), event()
        vec.memset(T.z[:], 1.0).then_inc(e_one, 1)
        g.wait_ge(e_one, 1)
        g.affine_select(T.z[:], T.z[:], [[-1, ZW]], AluOpType.is_equal, 0.0, 3, 4).then_inc(e_diag, 1)
        vec.wait_ge(e_diag, 1)
        for t in range(4):
            e = event()
            vec.quantize_mx(T.wq[:, cols(t)], T.wsc[:, cols(t)], T.z[:, 3 - t:3 - t + E]).then_inc(e, 1)
            w_ready.append(e)

    e_b = event()
    vec.wait_ge(T.sem.ldb, 16)
    vec.quantize_mx(T.bq[:], T.bsc[:], T.bt[:]).then_inc(e_b, 1)
    e_a = []
    for i in range(4):
        if i == 0:
            vec.wait_ge(T.sem.lda0, 16)
        if i == 3:
            vec.wait_ge(T.sem.lda1, 16)
        e_a.append(event())
        vec.quantize_mx(T.aq[:, cols(i)], T.asc[:, cols(i)], T.at[:, E * i:E * i + E]).then_inc(e_a[i], 1)
    ten.wait_ge(e_b, 1)
    seen = [0]

    def product(ps, i, stop):
        if seen[0] == i:
            ten.wait_ge(e_a[i], 1)
            seen[0] += 1
        for k in range(2):
            m = ten.matmul_mx(bank(ps, i), T.aq[:, cols(i)], T.asc[:, cols(i)], T.bq[:, cols(k)], T.bsc[:, cols(k)],
                              k == 0, stop and k == 1)
        return m

    def add(ps, t, k, stop):
        return ten.matmul_mx(bank(ps, t), T.wq[:, cols(t)], T.wsc[:, cols(t)], T["rq%s" % k][:], T["rsc%s" % k][:],
                             False, stop)

    def mark(m):
        e = event()
        m.then_inc(e, 1)
        return e

    def drain(dst, ps, done, engines):
        out = []
        for t in range(4):
            d = dst[:, t:E:4]
            if engines[t] == "v":
                vec.wait_ge(done[t], 1)
                c = vec.tensor_copy(d, bank(ps, t))
            else:
                sca.wait_ge(done[t], 1)
                c = sca.activation(d, bank(ps, t), ActivationFunctionType.Copy)
            out.append(mark(c))
        return out

    def engines_to(dsts):
        mask = -1
        for d in dsts:
            mask &= topo.mask(core, d)
        return mask

    arrivals = 2 * bin(engines_to([c for c in T.cores if c != core])).count("1")

    def send(q, sc, name, group):
        dsts = [T.cores[d] for d in group]
        mask = engines_to(dsts)
        ids = []
        for d in dsts:
            rid, pid, _ = topo.addr(d)
            ids.append(DstId(rid=rid, pnc=pid))
        sem = T.sem["arr%s" % name]
        for src, land in ((q[:].bitcast(dt.uint8), T["rq%s" % name][:].bitcast(dt.uint8)),
                          (sc[:], T["rsc%s" % name][:])):
            if len(ids) == 1:
                g.remote_dma(land, src, sem, T.sem.sent, ids[0].pnc, ids[0].rid, mask)
            else:
                g.remote_dma_fused([RemoteDMATransfer(dst_ids=ids, dma_engine_mask=mask, remote_sem=sem,
                                                      srcs=[src], dsts=[land] * len(ids))], local_sem=T.sem.sent)
            sent[0] += bin(mask).count("1")

    def pack(h, q, sc, copies):
        for c in copies:
            vec.wait_ge(c, 1)
        g.wait_ge(mark(vec.quantize_mx(q[:], sc[:], h[:])), 1)

    copies = []
    if rank in SEND_R:
        done = [mark(product(T.ps0, i, True)) for i in range(4)]
        copies = drain(T.h, T.ps0, done, "sssv")
        pack(T.h, T.hq, T.hsc, copies)
        for group in SEND_R[rank]:
            send(T.hq, T.hsc, rank, group)

    if tiles_in:
        sums = T.ps1 if copies else T.ps0
        relay, dst = HUB.get(rank, ([], None))
        apart = relay and relay != tiles_in
        for i in range(4):
            product(sums, i, False)
        if apart:
            for i in range(4):
                ten.wait_ge(copies[i], 1)
                product(T.ps0, i, False)
        for e in w_ready:
            ten.wait_ge(e, 1)
        for n, k in enumerate(tiles_in):
            ten.wait_ge(T.sem["arr%s" % k], arrivals)
            last = n == len(tiles_in) - 1
            if apart and k in relay:
                rdone = [mark(add(sums, t, k, True)) for t in range(4)]
                for t in range(4):
                    add(T.ps0, t, k, False)
            elif last:
                done = [mark(add(T.ps0 if apart else sums, t, k, True)) for t in range(4)]
            else:
                for t in range(4):
                    add(T.ps0 if apart else sums, t, k, False)
        if relay:
            pack(T.h2, T.h2q, T.h2sc, drain(T.h2, sums, rdone if apart else done, "svsv"))
            send(T.h2q, T.h2sc, "s", [dst])
        final = T.ps0 if apart else sums
    else:
        final = T.ps0

    for e in drain(T.ysb, final, done, "svsv"):
        syn.wait_ge(e, 1)
    syn.dma_start(T.y[:], T.ysb[:]).then_inc(T.sem.stored, 16)
    syn.wait_ge(T.sem.stored, 16)
    if sent[0]:
        g.wait_ge(T.sem.sent, sent[0])
